import numpy as np
import ml_dtypes


def mxq(x, axis, fmt="e4m3"):
    dtype, down = {"e4m3": (ml_dtypes.float8_e4m3fn, 7), "e5m2": (ml_dtypes.float8_e5m2, 14)}[fmt]
    v = np.moveaxis(np.asarray(x, np.float32).astype(ml_dtypes.bfloat16).astype(np.float64), axis, -1)
    blocks = v.reshape(v.shape[:-1] + (-1, 32))
    amax = np.abs(blocks).max(-1, keepdims=True)
    byte = np.maximum(np.where(amax > 0, np.frexp(amax)[1] - 1 + 127, 0) - down, 1)
    scale = np.exp2(byte - 127.0)
    codes = (blocks / scale).astype(np.float32).astype(dtype).astype(np.float64)
    return np.moveaxis((codes * scale).reshape(v.shape), -1, axis)


WIDE = False


def mx_kscale(k):
    if not WIDE:
        return np.ones(k)
    levels = np.array([10, -10, 5, -5, 0])
    if k % 512:
        return np.exp2(np.random.permutation(np.resize(levels, k // 32))).repeat(32)
    a = np.empty((k // 512, 16))
    for p in range(k // 512):
        a[p, :8] = np.random.permutation(np.resize(levels, 8))
        for g in range(8):
            far = levels[np.abs(levels - a[p, g]) >= 10]
            a[p, g + 8] = far[np.random.randint(len(far))]
    return np.exp2(a.ravel()).repeat(32)


def f64(x):
    return np.asarray(x).astype(np.float64)


def striped(idx):
    return np.tile(np.asarray(idx).reshape(-1, 16).T, (8, 1)).astype(np.uint16)


def unstriped(offs):
    return offs[:16].T.reshape(-1).astype(np.int64)


def striped8(idx):
    return np.asarray(idx).reshape(8, -1, 16).transpose(0, 2, 1).reshape(128, -1).astype(np.uint16)


def unstriped8(offs):
    return offs.reshape(8, 16, -1).transpose(0, 2, 1).reshape(8, -1).astype(np.int64)


def pick8(x, idx, run):
    r = np.arange(len(x))
    return x[r[:, None], idx[r % (8 * run) // run]]


E2M1 = np.array([0.0, 0.5, 1.0, 1.5, 2.0, 3.0, 4.0, 6.0, -0.0, -0.5, -1.0, -1.5, -2.0, -3.0, -4.0, -6.0])


def pack_weight(w, fmt):
    k, n = w.shape
    w = f64(np.asarray(w, np.float32).astype(ml_dtypes.bfloat16)).reshape(k // 32, 32, n)
    amax = np.abs(w).max(1)
    if fmt == "e4m3":
        byte = np.frexp(amax)[1] - 1 + 127 - 7
    else:
        mant, ex = np.frexp(amax / 6.0)
        byte = np.where(mant > 0.5, ex, ex - 1) + 127
    byte = np.clip(np.where(amax > 0, byte, 1), 1, 254)
    scaled = (w * np.exp2(127.0 - byte)[:, None, :]).reshape(k, n).astype(np.float32)
    by_word = np.ascontiguousarray(scaled.reshape(k // 512, 128, 4, n).transpose(0, 1, 3, 2))
    if fmt == "e4m3":
        words = by_word.astype(ml_dtypes.float8_e4m3fn).view(np.uint8)
    else:
        c = by_word.astype(ml_dtypes.float4_e2m1fn).view(np.uint8) & 0xF
        words = (c[..., 0::2] | (c[..., 1::2] << 4)).reshape(k // 512, 128, 2 * n)
    return np.ascontiguousarray(words), np.ascontiguousarray(byte.astype(np.uint8).reshape(k // 512, 16, n))


def unpack_weight(words, scales, fmt):
    g, _, n = scales.shape
    words = np.ascontiguousarray(words).reshape(g, 128, n, -1)
    if fmt == "e4m3":
        vals = words.view(ml_dtypes.float8_e4m3fn).astype(np.float64)
    else:
        nib = np.empty((g, 128, n, 4), np.uint8)
        nib[..., 0::2] = words & 0xF
        nib[..., 1::2] = words >> 4
        vals = E2M1[nib]
    vals = vals * np.repeat(np.exp2(scales.astype(np.float64) - 127.0), 8, axis=1)[..., None]
    return vals.transpose(0, 1, 3, 2).reshape(g * 512, n)


def sgn(shape):
    return np.random.uniform(0.5, 2.0, shape) * np.where(np.random.standard_normal(shape) < 0, -1.0, 1.0)


K, J, R, T, F, G, O, N, U, E = 512, 512, 512, 2048, 2048, 2048, 256, 256, 128, 512


def setup_inputs():
    n = np.random.standard_normal
    idx = np.random.permutation(T)[:J]
    idx2 = np.random.permutation(F)[:R]
    idx3 = np.stack([np.random.permutation(G)[:R] for _ in range(8)])
    idx4 = np.stack([np.random.permutation(J)[:O] for _ in range(8)])
    idx5 = np.random.permutation(T)[:O]
    idx6 = np.stack([np.random.permutation(O)[:U] for _ in range(8)])
    idx7 = np.stack([np.random.permutation(E)[:U] for _ in range(8)])
    fk = mx_kscale(K)
    fr = mx_kscale(R)
    xtp = pack_weight(n((K, T)) * fk[:, None], "e2m1")
    wbp = pack_weight(n((R, N)) * 1 / np.sqrt(R) / fr[:, None], "e2m1")
    wsp = pack_weight(n((K, N)) * 1 / np.sqrt(K) / fk[:, None], "e4m3")
    return {
        "xt_words": xtp[0],
        "xt_scales": xtp[1],
        "ua": (np.random.randint(-7, 8, (K, F)).astype(np.float64)).astype(np.float32),
        "ub": (np.random.randint(-7, 8, (K, G)).astype(np.float64)).astype(np.float32),
        "ha": ((np.random.randint(10, 25, (K, 1)) / 1024.0) / fk[:, None]).astype(np.float32),
        "hb": ((np.random.randint(4, 13, (K, 1)) / 1024.0) / fk[:, None]).astype(np.float32),
        "sa": (np.random.uniform(0.5, 1.6, (R, 1)) * fr[:, None]).astype(np.float32),
        "wb_words": wbp[0],
        "wb_scales": wbp[1],
        "ws_words": wsp[0],
        "ws_scales": wsp[1],
        "so": (sgn((N, 1))).astype(np.float32),
        "offs": striped(idx),
        "offs2": striped(idx2),
        "offs3": striped8(idx3),
        "offs4": striped8(idx4),
        "offs5": striped(idx5),
        "offs6": striped8(idx6),
        "offs7": striped8(idx7),
    }


def reference(xt_words, xt_scales, ua, ub, ha, hb, sa, wb_words, wb_scales, ws_words, ws_scales, so, offs, offs2, offs3, offs4, offs5, offs6, offs7):
    idx = unstriped(offs)
    idx2 = unstriped(offs2)
    idx3 = unstriped8(offs3)
    idx4 = unstriped8(offs4)
    idx5 = unstriped(offs5)
    idx6 = unstriped8(offs6)
    idx7 = unstriped8(offs7)
    xtu = unpack_weight(xt_words, xt_scales, "e2m1")
    wbu = unpack_weight(wb_words, wb_scales, "e2m1")
    wsu = unpack_weight(ws_words, ws_scales, "e4m3")
    wc = f64(ua)[:, idx2] * f64(ha) + pick8(f64(ub), idx3, 64) * f64(hb)
    wcq = mxq(wc, 0, "e4m3")
    xtidxg = xtu[:, idx]
    a = wcq.T @ xtidxg
    g1 = np.maximum(a, 0.0)
    hid = pick8(g1, idx4, 64) * f64(sa)
    hidq = mxq(hid, 0, "e4m3")
    xtidx5g = xtu[:, idx5]
    p = wbu.T @ hidq + wsu.T @ xtidx5g
    m0 = pick8(p, idx6, 16) * f64(so)
    y = np.zeros((N, E))
    y[np.arange(N)[:, None], idx7[np.arange(N) % 128 // 16]] = m0
    return y

@@ -1,0 +1,222 @@
+from contextlib import ExitStack
+
+import concourse.mybir as mybir
+
+K, J, R, T, F, G, O, N, U, E = 512, 512, 512, 2048, 2048, 2048, 256, 256, 128, 512
+FLOPS = 2 * K * R * J + 2 * R * N * O + 2 * K * N * O
+
+F32 = mybir.dt.float32
+BF16 = mybir.dt.bfloat16
+I32 = mybir.dt.int32
+U32 = mybir.dt.uint32
+U16 = mybir.dt.uint16
+U8 = mybir.dt.uint8
+FP8X4 = mybir.dt.float8_e4m3fn_x4
+FP4X4 = mybir.dt.float4_e2m1fn_x4
+ACT = mybir.ActivationFunctionType
+ALU = mybir.AluOpType
+
+P = 128
+PACK = 4
+PER_COL = 16
+SCALE_ROWS = 16
+ROW_STEP = P // SCALE_ROWS
+
+
+def tile_picked_tokens_basedetail_one_kept_further_posted_kernel(
+    tc, xt_words, xt_scales, ua, ub, ha, hb, sa, wb_words, wb_scales, ws_words, ws_scales, so,
+    offs, offs2, offs3, offs4, offs5, offs6, offs7, out,
+):
+    nc = tc.nc
+    with ExitStack() as ctx:
+        sb = ctx.enter_context(tc.tile_pool(name="sb", bufs=1))
+        a_psum = ctx.enter_context(tc.psum_pool(name="a_psum", bufs=4))
+        p_psum = ctx.enter_context(tc.psum_pool(name="p_psum", bufs=1))
+
+        def tile(shape, dtype, name):
+            return sb.tile(shape, dtype, name=name, align_bytes=64)
+
+        def load_list(src, name):
+            dst = sb.tile(list(src.shape), U16, name=name)
+            nc.sync.dma_start(dst[:], src)
+            return dst
+
+        def load_by_word(src, name):
+            dst = tile([P, PACK], F32, name)
+            nc.sync.dma_start(dst[:], src.rearrange("(p j) o -> p (j o)", j=PACK))
+            return dst
+
+        def load_rows(src, j, name):
+            dst = tile([P, src.shape[1]], F32, name)
+            nc.sync.dma_start(dst[:], src.rearrange("(p j) c -> j p c", j=PACK)[j])
+            return dst
+
+        def load_scale_plane(src, plane):
+            for q in range(4):
+                nc.sync.dma_start(plane[32 * q : 32 * q + 4, :].bitcast(I32), src[0, 4 * q : 4 * q + 4, :].bitcast(I32))
+
+        xt_scale_window = tile([P, T], U8, "xt_scale_window")
+        x_plane = tile([P, J + O], U8, "x_plane")
+        ws_plane = tile([P, N], U8, "ws_plane")
+        wb_plane = tile([P, N], U8, "wb_plane")
+        for plane in (xt_scale_window, x_plane, ws_plane, wb_plane):
+            nc.vector.memset(plane[:].bitcast(I32), 0)
+        pages = [tile([P, E], F32, f"page{b}") for b in range(N // P)]
+        for page in pages:
+            nc.vector.memset(page[:], 0.0)
+
+        ua_rows, ub_rows = [], []
+        ub_rows.append(load_rows(ub, 0, "ub0"))
+        list3 = load_list(offs3, "list3")
+        hb_sb = load_by_word(hb, "hb_sb")
+        ua_rows.append(load_rows(ua, 0, "ua0"))
+        list2 = load_list(offs2, "list2")
+        ha_sb = load_by_word(ha, "ha_sb")
+        xt_word_window = tile([P, T], U16, "xt_word_window")
+        nc.sync.dma_start(xt_word_window[:].bitcast(I32), xt_words[0].bitcast(I32))
+        list1 = load_list(offs, "list1")
+        ub_rows.append(load_rows(ub, 1, "ub1"))
+        nc.sync.dma_start(xt_scale_window[0:P:ROW_STEP, :].bitcast(I32), xt_scales[0].bitcast(I32))
+        list5 = load_list(offs5, "list5")
+        ua_rows.append(load_rows(ua, 1, "ua1"))
+        for j in range(2, PACK):
+            ub_rows.append(load_rows(ub, j, f"ub{j}"))
+            ua_rows.append(load_rows(ua, j, f"ua{j}"))
+        list4 = load_list(offs4, "list4")
+        sa_sb = load_by_word(sa, "sa_sb")
+        ws_codes = tile([P, N], U32, "ws_codes")
+        nc.sync.dma_start(ws_codes[:].bitcast(I32), ws_words[0].rearrange("p n t -> p (n t)").bitcast(I32))
+        load_scale_plane(ws_scales, ws_plane)
+        wb_codes = tile([P, N], U16, "wb_codes")
+        nc.sync.dma_start(wb_codes[:].bitcast(I32), wb_words[0].bitcast(I32))
+        load_scale_plane(wb_scales, wb_plane)
+        list6 = load_list(offs6, "list6")
+        so_sb = tile([P, N // P], F32, "so_sb")
+        with nc.allow_non_contiguous_dma(reason="one weight a partition"):
+            nc.sync.dma_start(so_sb[:], so.rearrange("(b p) o -> p (b o)", p=P))
+        list7 = load_list(offs7, "list7")
+
+        x_codes = tile([P, J], U16, "x_codes")
+        x5_codes = tile([P, O], U16, "x5_codes")
+        x_bytes = tile([P, J + O], U8, "x_bytes")
+        nc.vector.tensor_copy(x_bytes[:, :J], xt_scale_window[:].indirect(list1[:]))
+        nc.vector.tensor_copy(x_bytes[:, J:], xt_scale_window[:].indirect(list5[:]))
+        nc.vector.tensor_copy(x_codes[:], xt_word_window[:].indirect(list1[:]))
+        nc.vector.tensor_copy(x5_codes[:], xt_word_window[:].indirect(list5[:]))
+        for q in range(4):
+            nc.gpsimd.dma_start(
+                x_plane[32 * q : 32 * q + 4, :].bitcast(I32), x_bytes[32 * q : 32 * q + 32 : ROW_STEP, :].bitcast(I32)
+            )
+
+        wc = tile([P, PACK * R], BF16, "wc")
+        wc_pairs = wc[:].rearrange("p (t m i j) -> p m t i j", t=PACK, i=2, j=PACK)
+        wc_tiles = wc[:].rearrange("p (t m j) -> p t m j", t=PACK, j=PACK)
+
+        def fetch(dst, window, lst, scale, lo, hi):
+            nc.scalar.activation(
+                out=dst, in_=window[:].indirect(lst[:, lo // PER_COL : hi // PER_COL]), func=ACT.Copy, scale=scale
+            )
+
+        def add_range(base, detail, j, lo, hi):
+            pattern = "p (m i t) -> p m t i"
+            nc.vector.tensor_tensor(
+                out=wc_pairs[:, lo // 8 : hi // 8, :, :, j],
+                in0=base[:, lo:hi].rearrange(pattern, i=2, t=PACK),
+                in1=detail[:, lo:hi].rearrange(pattern, i=2, t=PACK),
+                op=ALU.add,
+            )
+
+        def add_tile(base, detail, j, t, lo, hi):
+            nc.vector.tensor_tensor(
+                out=wc_tiles[:, t, lo // PACK : hi // PACK, j],
+                in0=base[:, lo + t : hi : PACK],
+                in1=detail[:, lo + t : hi : PACK],
+                op=ALU.add,
+            )
+
+        wc_codes = [tile([P, P], U32, f"wc_codes{t}") for t in range(PACK)]
+        wc_plane = [tile([P, P], U8, f"wc_plane{t}") for t in range(PACK)]
+
+        def quantize_wc(t):
+            nc.vector.quantize_mx(
+                out=wc_codes[t][:].bitcast(FP8X4), scales=wc_plane[t][:], in_=wc[:, t * R : (t + 1) * R]
+            )
+
+        last = PACK - 1
+        for j in range(PACK):
+            base = tile([P, R], F32, f"base{j}")
+            detail = tile([P, R], F32, f"detail{j}")
+            fetch(detail[:], ub_rows[j], list3, hb_sb[:, j : j + 1], 0, R)
+            if j < last:
+                fetch(base[:], ua_rows[j], list2, ha_sb[:, j : j + 1], 0, R)
+                add_range(base, detail, j, 0, R)
+            else:
+                for lo, hi in ((0, R // 4), (R // 4, R // 2), (R // 2, R)):
+                    fetch(base[:, lo:hi], ua_rows[j], list2, ha_sb[:, j : j + 1], lo, hi)
+                add_range(base, detail, j, 0, R // 4)
+                add_range(base, detail, j, R // 4, R // 2)
+                add_tile(base, detail, j, 0, R // 2, R)
+                for t in range(1, PACK):
+                    add_tile(base, detail, j, t, R // 2, R)
+                    quantize_wc(t - 1)
+                quantize_wc(last)
+
+        HALF_J = J // 2
+        HALF_O = O // 2
+        hid_planes = tile([P, PACK * O], BF16, "hid_planes")
+        for t in range(PACK):
+            g1 = tile([P, J], F32, f"g1_{t}")
+            for lo in range(0, J, HALF_J):
+                cols = slice(lo, lo + HALF_J)
+                acc = a_psum.tile([P, HALF_J], F32, name="acc")
+                nc.tensor.matmul_mx(
+                    out=acc[:], lhsT=wc_codes[t][:].bitcast(FP8X4), lhsT_scale=wc_plane[t][:],
+                    rhs=x_codes[:, cols].bitcast(FP4X4), rhs_scale=x_plane[:, cols], start=True, stop=True,
+                )
+                if t == 0:
+                    nc.scalar.activation(out=g1[:, cols], in_=acc[:], func=ACT.Relu)
+                else:
+                    nc.vector.tensor_scalar_max(g1[:, cols], acc[:], 0.0)
+            cuts = ((0, O),) if t < last else ((0, HALF_O), (HALF_O, O))
+            for lo, hi in cuts:
+                fetch(hid_planes[:, t * O + lo : t * O + hi], g1, list4, sa_sb[:, t : t + 1], lo, hi)
+
+        sums = {}
+        for h in range(2):
+            for b in range(N // P):
+                sums[b, h] = p_psum.tile([P, HALF_O], F32, name=f"sum{b}_{h}")
+                cols = slice(h * HALF_O, (h + 1) * HALF_O)
+                nc.tensor.matmul_mx(
+                    out=sums[b, h][:], lhsT=ws_codes[:, b * P : (b + 1) * P].bitcast(FP8X4),
+                    lhsT_scale=ws_plane[:, b * P : (b + 1) * P],
+                    rhs=x5_codes[:, cols].bitcast(FP4X4),
+                    rhs_scale=x_plane[:, J + h * HALF_O : J + (h + 1) * HALF_O], start=True, stop=False,
+                )
+        hid_by_place = hid_planes[:].rearrange("p (t o) -> p o t", t=PACK)
+        hid = [tile([P, HALF_O, PACK], BF16, f"hid{h}") for h in range(2)]
+        for h in range(2):
+            nc.vector.tensor_copy(hid[h][:], hid_by_place[:, h * HALF_O : (h + 1) * HALF_O, :])
+        p_rows = [tile([P, O], F32, f"p_rows{b}") for b in range(N // P)]
+        for h in range(2):
+            hid_codes = tile([P, HALF_O], U32, f"hid_codes{h}")
+            hid_plane = tile([P, HALF_O], U8, f"hid_plane{h}")
+            nc.vector.quantize_mx(
+                out=hid_codes[:].bitcast(FP8X4), scales=hid_plane[:], in_=hid[h][:].rearrange("p o t -> p (o t)")
+            )
+            cols = slice(h * HALF_O, (h + 1) * HALF_O)
+            for b in range(N // P):
+                nc.tensor.matmul_mx(
+                    out=sums[b, h][:], lhsT=wb_codes[:, b * P : (b + 1) * P].bitcast(FP4X4),
+                    lhsT_scale=wb_plane[:, b * P : (b + 1) * P],
+                    rhs=hid_codes[:].bitcast(FP8X4), rhs_scale=hid_plane[:], start=False, stop=True,
+                )
+                if (b, h) == (1, 1):
+                    nc.vector.tensor_copy(p_rows[b][:, cols], sums[b, h][:])
+                else:
+                    nc.scalar.copy(p_rows[b][:, cols], sums[b, h][:])
+
+        for b in range(N // P):
+            ends = tile([P, U], F32, f"ends{b}")
+            fetch(ends[:], p_rows[b], list6, so_sb[:, b : b + 1], 0, U)
+            nc.vector.tensor_copy(pages[b][:].indirect(list7[:]), ends[:])
+            nc.sync.dma_start(out[b * P : (b + 1) * P, :], pages[b][:])

@@ -21,6 +21,7 @@ PACK = 4
 PER_COL = 16
 SCALE_ROWS = 16
 ROW_STEP = P // SCALE_ROWS
+EARLY = 192
 
 
 def tile_picked_tokens_basedetail_one_kept_further_posted_kernel(
@@ -30,8 +31,7 @@ def tile_picked_tokens_basedetail_one_kept_further_posted_kernel(
     nc = tc.nc
     with ExitStack() as ctx:
         sb = ctx.enter_context(tc.tile_pool(name="sb", bufs=1))
-        a_psum = ctx.enter_context(tc.psum_pool(name="a_psum", bufs=4))
-        p_psum = ctx.enter_context(tc.psum_pool(name="p_psum", bufs=1))
+        psum = ctx.enter_context(tc.psum_pool(name="psum", bufs=8))
 
         def tile(shape, dtype, name):
             return sb.tile(shape, dtype, name=name, align_bytes=64)
@@ -69,15 +69,15 @@ def tile_picked_tokens_basedetail_one_kept_further_posted_kernel(
         ub_rows.append(load_rows(ub, 0, "ub0"))
         list3 = load_list(offs3, "list3")
         hb_sb = load_by_word(hb, "hb_sb")
+        list1 = load_list(offs, "list1")
         ua_rows.append(load_rows(ua, 0, "ua0"))
+        nc.sync.dma_start(xt_scale_window[0:P:ROW_STEP, :].bitcast(I32), xt_scales[0].bitcast(I32))
+        list5 = load_list(offs5, "list5")
         list2 = load_list(offs2, "list2")
+        ub_rows.append(load_rows(ub, 1, "ub1"))
         ha_sb = load_by_word(ha, "ha_sb")
         xt_word_window = tile([P, T], U16, "xt_word_window")
         nc.sync.dma_start(xt_word_window[:].bitcast(I32), xt_words[0].bitcast(I32))
-        list1 = load_list(offs, "list1")
-        ub_rows.append(load_rows(ub, 1, "ub1"))
-        nc.sync.dma_start(xt_scale_window[0:P:ROW_STEP, :].bitcast(I32), xt_scales[0].bitcast(I32))
-        list5 = load_list(offs5, "list5")
         ua_rows.append(load_rows(ua, 1, "ua1"))
         for j in range(2, PACK):
             ub_rows.append(load_rows(ub, j, f"ub{j}"))
@@ -108,30 +108,16 @@ def tile_picked_tokens_basedetail_one_kept_further_posted_kernel(
                 x_plane[32 * q : 32 * q + 4, :].bitcast(I32), x_bytes[32 * q : 32 * q + 32 : ROW_STEP, :].bitcast(I32)
             )
 
-        wc = tile([P, PACK * R], BF16, "wc")
-        wc_pairs = wc[:].rearrange("p (t m i j) -> p m t i j", t=PACK, i=2, j=PACK)
-        wc_tiles = wc[:].rearrange("p (t m j) -> p t m j", t=PACK, j=PACK)
+        wc = [tile([P, P, PACK], BF16, f"wc{t}") for t in range(PACK)]
 
         def fetch(dst, window, lst, scale, lo, hi):
             nc.scalar.activation(
                 out=dst, in_=window[:].indirect(lst[:, lo // PER_COL : hi // PER_COL]), func=ACT.Copy, scale=scale
             )
 
-        def add_range(base, detail, j, lo, hi):
-            pattern = "p (m i t) -> p m t i"
+        def add_tile(base_cols, detail, j, t, lo, hi):
             nc.vector.tensor_tensor(
-                out=wc_pairs[:, lo // 8 : hi // 8, :, :, j],
-                in0=base[:, lo:hi].rearrange(pattern, i=2, t=PACK),
-                in1=detail[:, lo:hi].rearrange(pattern, i=2, t=PACK),
-                op=ALU.add,
-            )
-
-        def add_tile(base, detail, j, t, lo, hi):
-            nc.vector.tensor_tensor(
-                out=wc_tiles[:, t, lo // PACK : hi // PACK, j],
-                in0=base[:, lo + t : hi : PACK],
-                in1=detail[:, lo + t : hi : PACK],
-                op=ALU.add,
+                out=wc[t][:, lo // PACK : hi // PACK, j], in0=base_cols, in1=detail[:, lo + t : hi : PACK], op=ALU.add
             )
 
         wc_codes = [tile([P, P], U32, f"wc_codes{t}") for t in range(PACK)]
@@ -139,36 +125,43 @@ def tile_picked_tokens_basedetail_one_kept_further_posted_kernel(
 
         def quantize_wc(t):
             nc.vector.quantize_mx(
-                out=wc_codes[t][:].bitcast(FP8X4), scales=wc_plane[t][:], in_=wc[:, t * R : (t + 1) * R]
+                out=wc_codes[t][:].bitcast(FP8X4), scales=wc_plane[t][:], in_=wc[t][:].rearrange("p m j -> p (m j)")
             )
 
         last = PACK - 1
         for j in range(PACK):
-            base = tile([P, R], F32, f"base{j}")
             detail = tile([P, R], F32, f"detail{j}")
             fetch(detail[:], ub_rows[j], list3, hb_sb[:, j : j + 1], 0, R)
-            if j < last:
-                fetch(base[:], ua_rows[j], list2, ha_sb[:, j : j + 1], 0, R)
-                add_range(base, detail, j, 0, R)
-            else:
-                for lo, hi in ((0, R // 4), (R // 4, R // 2), (R // 2, R)):
-                    fetch(base[:, lo:hi], ua_rows[j], list2, ha_sb[:, j : j + 1], lo, hi)
-                add_range(base, detail, j, 0, R // 4)
-                add_range(base, detail, j, R // 4, R // 2)
-                add_tile(base, detail, j, 0, R // 2, R)
-                for t in range(1, PACK):
-                    add_tile(base, detail, j, t, R // 2, R)
-                    quantize_wc(t - 1)
-                quantize_wc(last)
+            edges = (0, R) if j < last else (0, EARLY, R)
+            for lo, hi in zip(edges, edges[1:]):
+                base = tile([P, hi - lo], F32, f"base{j}_{lo}")
+                fetch(base[:], ua_rows[j], list2, ha_sb[:, j : j + 1], lo, hi)
+                by_tile = base[:].rearrange("p (m t) -> p t m", t=PACK)
+                if j == last and hi == R:
+                    dealt = tile([P, 2, (hi - lo) // PACK], F32, "dealt")
+                    nc.scalar.copy(dealt[:], by_tile[:, 2:, :])
+                    for pair in range(2):
+                        for t in (2 * pair, 2 * pair + 1):
+                            add_tile(dealt[:, t - 2, :] if pair else by_tile[:, t, :], detail, j, t, lo, hi)
+                        for t in (2 * pair, 2 * pair + 1):
+                            quantize_wc(t)
+                else:
+                    for t in range(PACK):
+                        add_tile(by_tile[:, t, :], detail, j, t, lo, hi)
 
-        HALF_J = J // 2
         HALF_O = O // 2
         hid_planes = tile([P, PACK * O], BF16, "hid_planes")
         for t in range(PACK):
             g1 = tile([P, J], F32, f"g1_{t}")
-            for lo in range(0, J, HALF_J):
-                cols = slice(lo, lo + HALF_J)
-                acc = a_psum.tile([P, HALF_J], F32, name="acc")
+            if t == 0:
+                edges = (0, J // 4, J // 2, 3 * J // 4, J)
+            elif t < last:
+                edges = (0, J // 2, J)
+            else:
+                edges = (0, J // 2, 3 * J // 4, J)
+            for lo, hi in zip(edges, edges[1:]):
+                cols = slice(lo, hi)
+                acc = psum.tile([P, hi - lo], F32, name="bank")
                 nc.tensor.matmul_mx(
                     out=acc[:], lhsT=wc_codes[t][:].bitcast(FP8X4), lhsT_scale=wc_plane[t][:],
                     rhs=x_codes[:, cols].bitcast(FP4X4), rhs_scale=x_plane[:, cols], start=True, stop=True,
@@ -184,7 +177,7 @@ def tile_picked_tokens_basedetail_one_kept_further_posted_kernel(
         sums = {}
         for h in range(2):
             for b in range(N // P):
-                sums[b, h] = p_psum.tile([P, HALF_O], F32, name=f"sum{b}_{h}")
+                sums[b, h] = psum.tile([P, HALF_O], F32, name="bank")
                 cols = slice(h * HALF_O, (h + 1) * HALF_O)
                 nc.tensor.matmul_mx(
                     out=sums[b, h][:], lhsT=ws_codes[:, b * P : (b + 1) * P].bitcast(FP8X4),
@@ -194,8 +187,9 @@ def tile_picked_tokens_basedetail_one_kept_further_posted_kernel(
                 )
         hid_by_place = hid_planes[:].rearrange("p (t o) -> p o t", t=PACK)
         hid = [tile([P, HALF_O, PACK], BF16, f"hid{h}") for h in range(2)]
-        for h in range(2):
-            nc.vector.tensor_copy(hid[h][:], hid_by_place[:, h * HALF_O : (h + 1) * HALF_O, :])
+        nc.vector.tensor_copy(hid[1][:, :, :last], hid_by_place[:, HALF_O:, :last])
+        nc.vector.tensor_copy(hid[0][:], hid_by_place[:, :HALF_O, :])
+        nc.vector.tensor_copy(hid[1][:, :, last], hid_by_place[:, HALF_O:, last])
         p_rows = [tile([P, O], F32, f"p_rows{b}") for b in range(N // P)]
         for h in range(2):
             hid_codes = tile([P, HALF_O], U32, f"hid_codes{h}")
@@ -210,7 +204,7 @@ def tile_picked_tokens_basedetail_one_kept_further_posted_kernel(
                     lhsT_scale=wb_plane[:, b * P : (b + 1) * P],
                     rhs=hid_codes[:].bitcast(FP8X4), rhs_scale=hid_plane[:], start=False, stop=True,
                 )
-                if (b, h) == (1, 1):
+                if b == 1:
                     nc.vector.tensor_copy(p_rows[b][:, cols], sums[b, h][:])
                 else:
                     nc.scalar.copy(p_rows[b][:, cols], sums[b, h][:])

from contextlib import ExitStack

import concourse.mybir as mybir

K, J, R, T, F, G, O, N, U, E = 512, 512, 512, 2048, 2048, 2048, 256, 256, 128, 512
FLOPS = 2 * K * R * J + 2 * R * N * O + 2 * K * N * O

F32 = mybir.dt.float32
BF16 = mybir.dt.bfloat16
I32 = mybir.dt.int32
U32 = mybir.dt.uint32
U16 = mybir.dt.uint16
U8 = mybir.dt.uint8
FP8X4 = mybir.dt.float8_e4m3fn_x4
FP4X4 = mybir.dt.float4_e2m1fn_x4
ACT = mybir.ActivationFunctionType
ALU = mybir.AluOpType

P = 128
PACK = 4
PER_COL = 16
SCALE_ROWS = 16
ROW_STEP = P // SCALE_ROWS
EARLY = 192


def tile_picked_tokens_basedetail_one_kept_further_posted_kernel(
    tc, xt_words, xt_scales, ua, ub, ha, hb, sa, wb_words, wb_scales, ws_words, ws_scales, so,
    offs, offs2, offs3, offs4, offs5, offs6, offs7, out,
):
    nc = tc.nc
    with ExitStack() as ctx:
        sb = ctx.enter_context(tc.tile_pool(name="sb", bufs=1))
        psum = ctx.enter_context(tc.psum_pool(name="psum", bufs=8))

        def tile(shape, dtype, name):
            return sb.tile(shape, dtype, name=name, align_bytes=64)

        def load_list(src, name):
            dst = sb.tile(list(src.shape), U16, name=name)
            nc.sync.dma_start(dst[:], src)
            return dst

        def load_by_word(src, name):
            dst = tile([P, PACK], F32, name)
            nc.sync.dma_start(dst[:], src.rearrange("(p j) o -> p (j o)", j=PACK))
            return dst

        def load_rows(src, j, name):
            dst = tile([P, src.shape[1]], F32, name)
            nc.sync.dma_start(dst[:], src.rearrange("(p j) c -> j p c", j=PACK)[j])
            return dst

        def load_scale_plane(src, plane):
            for q in range(4):
                nc.sync.dma_start(plane[32 * q : 32 * q + 4, :].bitcast(I32), src[0, 4 * q : 4 * q + 4, :].bitcast(I32))

        xt_scale_window = tile([P, T], U8, "xt_scale_window")
        x_plane = tile([P, J + O], U8, "x_plane")
        ws_plane = tile([P, N], U8, "ws_plane")
        wb_plane = tile([P, N], U8, "wb_plane")
        for plane in (xt_scale_window, x_plane, ws_plane, wb_plane):
            nc.vector.memset(plane[:].bitcast(I32), 0)
        pages = [tile([P, E], F32, f"page{b}") for b in range(N // P)]
        for page in pages:
            nc.vector.memset(page[:], 0.0)

        ua_rows, ub_rows = [], []
        ub_rows.append(load_rows(ub, 0, "ub0"))
        list3 = load_list(offs3, "list3")
        hb_sb = load_by_word(hb, "hb_sb")
        list1 = load_list(offs, "list1")
        ua_rows.append(load_rows(ua, 0, "ua0"))
        nc.sync.dma_start(xt_scale_window[0:P:ROW_STEP, :].bitcast(I32), xt_scales[0].bitcast(I32))
        list5 = load_list(offs5, "list5")
        list2 = load_list(offs2, "list2")
        ub_rows.append(load_rows(ub, 1, "ub1"))
        ha_sb = load_by_word(ha, "ha_sb")
        xt_word_window = tile([P, T], U16, "xt_word_window")
        nc.sync.dma_start(xt_word_window[:].bitcast(I32), xt_words[0].bitcast(I32))
        ua_rows.append(load_rows(ua, 1, "ua1"))
        for j in range(2, PACK):
            ub_rows.append(load_rows(ub, j, f"ub{j}"))
            ua_rows.append(load_rows(ua, j, f"ua{j}"))
        list4 = load_list(offs4, "list4")
        sa_sb = load_by_word(sa, "sa_sb")
        ws_codes = tile([P, N], U32, "ws_codes")
        nc.sync.dma_start(ws_codes[:].bitcast(I32), ws_words[0].rearrange("p n t -> p (n t)").bitcast(I32))
        load_scale_plane(ws_scales, ws_plane)
        wb_codes = tile([P, N], U16, "wb_codes")
        nc.sync.dma_start(wb_codes[:].bitcast(I32), wb_words[0].bitcast(I32))
        load_scale_plane(wb_scales, wb_plane)
        list6 = load_list(offs6, "list6")
        so_sb = tile([P, N // P], F32, "so_sb")
        with nc.allow_non_contiguous_dma(reason="one weight a partition"):
            nc.sync.dma_start(so_sb[:], so.rearrange("(b p) o -> p (b o)", p=P))
        list7 = load_list(offs7, "list7")

        x_codes = tile([P, J], U16, "x_codes")
        x5_codes = tile([P, O], U16, "x5_codes")
        x_bytes = tile([P, J + O], U8, "x_bytes")
        nc.vector.tensor_copy(x_bytes[:, :J], xt_scale_window[:].indirect(list1[:]))
        nc.vector.tensor_copy(x_bytes[:, J:], xt_scale_window[:].indirect(list5[:]))
        nc.vector.tensor_copy(x_codes[:], xt_word_window[:].indirect(list1[:]))
        nc.vector.tensor_copy(x5_codes[:], xt_word_window[:].indirect(list5[:]))
        for q in range(4):
            nc.gpsimd.dma_start(
                x_plane[32 * q : 32 * q + 4, :].bitcast(I32), x_bytes[32 * q : 32 * q + 32 : ROW_STEP, :].bitcast(I32)
            )

        wc = [tile([P, P, PACK], BF16, f"wc{t}") for t in range(PACK)]

        def fetch(dst, window, lst, scale, lo, hi):
            nc.scalar.activation(
                out=dst, in_=window[:].indirect(lst[:, lo // PER_COL : hi // PER_COL]), func=ACT.Copy, scale=scale
            )

        def add_tile(base_cols, detail, j, t, lo, hi):
            nc.vector.tensor_tensor(
                out=wc[t][:, lo // PACK : hi // PACK, j], in0=base_cols, in1=detail[:, lo + t : hi : PACK], op=ALU.add
            )

        wc_codes = [tile([P, P], U32, f"wc_codes{t}") for t in range(PACK)]
        wc_plane = [tile([P, P], U8, f"wc_plane{t}") for t in range(PACK)]

        def quantize_wc(t):
            nc.vector.quantize_mx(
                out=wc_codes[t][:].bitcast(FP8X4), scales=wc_plane[t][:], in_=wc[t][:].rearrange("p m j -> p (m j)")
            )

        last = PACK - 1
        for j in range(PACK):
            detail = tile([P, R], F32, f"detail{j}")
            fetch(detail[:], ub_rows[j], list3, hb_sb[:, j : j + 1], 0, R)
            edges = (0, R) if j < last else (0, EARLY, R)
            for lo, hi in zip(edges, edges[1:]):
                base = tile([P, hi - lo], F32, f"base{j}_{lo}")
                fetch(base[:], ua_rows[j], list2, ha_sb[:, j : j + 1], lo, hi)
                by_tile = base[:].rearrange("p (m t) -> p t m", t=PACK)
                if j == last and hi == R:
                    dealt = tile([P, 2, (hi - lo) // PACK], F32, "dealt")
                    nc.scalar.copy(dealt[:], by_tile[:, 2:, :])
                    for pair in range(2):
                        for t in (2 * pair, 2 * pair + 1):
                            add_tile(dealt[:, t - 2, :] if pair else by_tile[:, t, :], detail, j, t, lo, hi)
                        for t in (2 * pair, 2 * pair + 1):
                            quantize_wc(t)
                else:
                    for t in range(PACK):
                        add_tile(by_tile[:, t, :], detail, j, t, lo, hi)

        HALF_O = O // 2
        hid_planes = tile([P, PACK * O], BF16, "hid_planes")
        for t in range(PACK):
            g1 = tile([P, J], F32, f"g1_{t}")
            if t == 0:
                edges = (0, J // 4, J // 2, 3 * J // 4, J)
            elif t < last:
                edges = (0, J // 2, J)
            else:
                edges = (0, J // 2, 3 * J // 4, J)
            for lo, hi in zip(edges, edges[1:]):
                cols = slice(lo, hi)
                acc = psum.tile([P, hi - lo], F32, name="bank")
                nc.tensor.matmul_mx(
                    out=acc[:], lhsT=wc_codes[t][:].bitcast(FP8X4), lhsT_scale=wc_plane[t][:],
                    rhs=x_codes[:, cols].bitcast(FP4X4), rhs_scale=x_plane[:, cols], start=True, stop=True,
                )
                if t == 0:
                    nc.scalar.activation(out=g1[:, cols], in_=acc[:], func=ACT.Relu)
                else:
                    nc.vector.tensor_scalar_max(g1[:, cols], acc[:], 0.0)
            cuts = ((0, O),) if t < last else ((0, HALF_O), (HALF_O, O))
            for lo, hi in cuts:
                fetch(hid_planes[:, t * O + lo : t * O + hi], g1, list4, sa_sb[:, t : t + 1], lo, hi)

        sums = {}
        for h in range(2):
            for b in range(N // P):
                sums[b, h] = psum.tile([P, HALF_O], F32, name="bank")
                cols = slice(h * HALF_O, (h + 1) * HALF_O)
                nc.tensor.matmul_mx(
                    out=sums[b, h][:], lhsT=ws_codes[:, b * P : (b + 1) * P].bitcast(FP8X4),
                    lhsT_scale=ws_plane[:, b * P : (b + 1) * P],
                    rhs=x5_codes[:, cols].bitcast(FP4X4),
                    rhs_scale=x_plane[:, J + h * HALF_O : J + (h + 1) * HALF_O], start=True, stop=False,
                )
        hid_by_place = hid_planes[:].rearrange("p (t o) -> p o t", t=PACK)
        hid = [tile([P, HALF_O, PACK], BF16, f"hid{h}") for h in range(2)]
        nc.vector.tensor_copy(hid[1][:, :, :last], hid_by_place[:, HALF_O:, :last])
        nc.vector.tensor_copy(hid[0][:], hid_by_place[:, :HALF_O, :])
        nc.vector.tensor_copy(hid[1][:, :, last], hid_by_place[:, HALF_O:, last])
        p_rows = [tile([P, O], F32, f"p_rows{b}") for b in range(N // P)]
        for h in range(2):
            hid_codes = tile([P, HALF_O], U32, f"hid_codes{h}")
            hid_plane = tile([P, HALF_O], U8, f"hid_plane{h}")
            nc.vector.quantize_mx(
                out=hid_codes[:].bitcast(FP8X4), scales=hid_plane[:], in_=hid[h][:].rearrange("p o t -> p (o t)")
            )
            cols = slice(h * HALF_O, (h + 1) * HALF_O)
            for b in range(N // P):
                nc.tensor.matmul_mx(
                    out=sums[b, h][:], lhsT=wb_codes[:, b * P : (b + 1) * P].bitcast(FP4X4),
                    lhsT_scale=wb_plane[:, b * P : (b + 1) * P],
                    rhs=hid_codes[:].bitcast(FP8X4), rhs_scale=hid_plane[:], start=False, stop=True,
                )
                if b == 1:
                    nc.vector.tensor_copy(p_rows[b][:, cols], sums[b, h][:])
                else:
                    nc.scalar.copy(p_rows[b][:, cols], sums[b, h][:])

        for b in range(N // P):
            ends = tile([P, U], F32, f"ends{b}")
            fetch(ends[:], p_rows[b], list6, so_sb[:, b : b + 1], 0, U)
            nc.vector.tensor_copy(pages[b][:].indirect(list7[:]), ends[:])
            nc.sync.dma_start(out[b * P : (b + 1) * P, :], pages[b][:])
